import numpy as np
import ml_dtypes


def mxq(x, axis, fmt="e4m3"):
    dtype, down = {"e4m3": (ml_dtypes.float8_e4m3fn, 7), "e5m2": (ml_dtypes.float8_e5m2, 14)}[fmt]
    v = np.moveaxis(np.asarray(x, np.float32).astype(ml_dtypes.bfloat16).astype(np.float64), axis, -1)
    blocks = v.reshape(v.shape[:-1] + (-1, 32))
    amax = np.abs(blocks).max(-1, keepdims=True)
    byte = np.maximum(np.where(amax > 0, np.frexp(amax)[1] - 1 + 127, 0) - down, 1)
    scale = np.exp2(byte - 127.0)
    codes = (blocks / scale).astype(np.float32).astype(dtype).astype(np.float64)
    return np.moveaxis((codes * scale).reshape(v.shape), -1, axis)


WIDE = False


def mx_kscale(k):
    if not WIDE:
        return np.ones(k)
    levels = np.array([10, -10, 5, -5, 0])
    if k % 512:
        return np.exp2(np.random.permutation(np.resize(levels, k // 32))).repeat(32)
    a = np.empty((k // 512, 16))
    for p in range(k // 512):
        a[p, :8] = np.random.permutation(np.resize(levels, 8))
        for g in range(8):
            far = levels[np.abs(levels - a[p, g]) >= 10]
            a[p, g + 8] = far[np.random.randint(len(far))]
    return np.exp2(a.ravel()).repeat(32)


def f64(x):
    return np.asarray(x).astype(np.float64)


def striped8(idx):
    return np.asarray(idx).reshape(8, -1, 16).transpose(0, 2, 1).reshape(128, -1).astype(np.uint16)


def unstriped8(offs):
    return offs.reshape(8, 16, -1).transpose(0, 2, 1).reshape(8, -1).astype(np.int64)


def pick8(x, idx, run):
    r = np.arange(len(x))
    return x[r[:, None], idx[r % (8 * run) // run]]


E2M1 = np.array([0.0, 0.5, 1.0, 1.5, 2.0, 3.0, 4.0, 6.0, -0.0, -0.5, -1.0, -1.5, -2.0, -3.0, -4.0, -6.0])


def pack_weight(w, fmt):
    k, n = w.shape
    w = f64(np.asarray(w, np.float32).astype(ml_dtypes.bfloat16)).reshape(k // 32, 32, n)
    amax = np.abs(w).max(1)
    if fmt == "e4m3":
        byte = np.frexp(amax)[1] - 1 + 127 - 7
    else:
        mant, ex = np.frexp(amax / 6.0)
        byte = np.where(mant > 0.5, ex, ex - 1) + 127
    byte = np.clip(np.where(amax > 0, byte, 1), 1, 254)
    scaled = (w * np.exp2(127.0 - byte)[:, None, :]).reshape(k, n).astype(np.float32)
    by_word = np.ascontiguousarray(scaled.reshape(k // 512, 128, 4, n).transpose(0, 1, 3, 2))
    if fmt == "e4m3":
        words = by_word.astype(ml_dtypes.float8_e4m3fn).view(np.uint8)
    else:
        c = by_word.astype(ml_dtypes.float4_e2m1fn).view(np.uint8) & 0xF
        words = (c[..., 0::2] | (c[..., 1::2] << 4)).reshape(k // 512, 128, 2 * n)
    return np.ascontiguousarray(words), np.ascontiguousarray(byte.astype(np.uint8).reshape(k // 512, 16, n))


def unpack_weight(words, scales, fmt):
    g, _, n = scales.shape
    words = np.ascontiguousarray(words).reshape(g, 128, n, -1)
    if fmt == "e4m3":
        vals = words.view(ml_dtypes.float8_e4m3fn).astype(np.float64)
    else:
        nib = np.empty((g, 128, n, 4), np.uint8)
        nib[..., 0::2] = words & 0xF
        nib[..., 1::2] = words >> 4
        vals = E2M1[nib]
    vals = vals * np.repeat(np.exp2(scales.astype(np.float64) - 127.0), 8, axis=1)[..., None]
    return vals.transpose(0, 1, 3, 2).reshape(g * 512, n)


D, T, I, Q = 512, 1024, 512, 128


def setup_inputs():
    n = np.random.standard_normal
    idx = np.stack([np.random.permutation(T)[:I] for _ in range(8)])
    idx2 = np.stack([np.random.permutation(T)[:I] for _ in range(8)])
    idx3 = np.stack([np.random.permutation(T)[:I] for _ in range(8)])
    fd = mx_kscale(D)
    keysp = pack_weight(n((D, T)) / fd[:, None], "e2m1")
    return {
        "query": (n((D, Q)) * 1.0 / np.sqrt(D) * fd[:, None]).astype(np.float32),
        "keys_words": keysp[0],
        "keys_scales": keysp[1],
        "old": (1.0 * n((Q, T))).astype(np.float32),
        "offs": striped8(idx),
        "offs2": striped8(idx2),
        "offs3": striped8(idx3),
    }


def reference(query, keys_words, keys_scales, old, offs, offs2, offs3):
    idx = unstriped8(offs)
    idx2 = unstriped8(offs2)
    idx3 = unstriped8(offs3)
    keysu = unpack_weight(keys_words, keys_scales, "e2m1")
    queryq = mxq(f64(query), 0, "e4m3")
    a = queryq.T @ keysu
    w = pick8(a, idx, 16) - pick8(a, idx2, 16)
    f1 = np.zeros((Q, T))
    f1[np.arange(Q)[:, None], idx3[np.arange(Q) % 128 // 16]] = w
    y = np.maximum(f1, f64(old)) + f64(old) * 0.25
    return y

@@ -1,0 +1,110 @@
+from contextlib import ExitStack
+
+import concourse.mybir as mybir
+
+D, T, I, Q = 512, 1024, 512, 128
+FLOPS = 2 * D * Q * T
+
+F32 = mybir.dt.float32
+BF16 = mybir.dt.bfloat16
+I32 = mybir.dt.int32
+U32 = mybir.dt.uint32
+U16 = mybir.dt.uint16
+U8 = mybir.dt.uint8
+FP8X4 = mybir.dt.float8_e4m3fn_x4
+FP4X4 = mybir.dt.float4_e2m1fn_x4
+ALU = mybir.AluOpType
+COPY = mybir.ActivationFunctionType.Copy
+
+P = 128
+PACK = 4
+SCORE_WIDTHS = (256, 256, 256, 128, 128)
+HALF = I // 2
+OUT_WIDTHS = (256, 256, 256, 128, 128)
+
+
+def tile_attend_difference_lean_largerput_heads_kernel(tc, query, keys_words, keys_scales, old, offs, offs2, offs3, out):
+    nc = tc.nc
+    with ExitStack() as ctx:
+        keep = ctx.enter_context(tc.tile_pool(name="keep", bufs=1))
+        psum = ctx.enter_context(tc.psum_pool(name="psum", bufs=1))
+
+        list1 = keep.tile([P, I // 16], U16, name="list1")
+        list2 = keep.tile([P, I // 16], U16, name="list2")
+        list3 = keep.tile([P, I // 16], U16, name="list3")
+        q_raw = keep.tile([P, PACK, Q], F32, name="q_raw")
+        q_bf = keep.tile([P, Q, PACK], BF16, name="q_bf", align_bytes=64)
+        q_codes = keep.tile([P, Q], U32, name="q_codes", align_bytes=64)
+        q_scales = keep.tile([P, Q], U8, name="q_scales", align_bytes=64)
+        k_words = keep.tile([P, 2 * T], U8, name="k_words", align_bytes=64)
+        k_scales = keep.tile([P, T], U8, name="k_scales", align_bytes=64)
+        old_sb = keep.tile([P, T], F32, name="old_sb")
+        scores = keep.tile([P, T], F32, name="scores")
+        placed = keep.tile([P, T], F32, name="placed")
+
+        nc.vector.memset(k_scales[:].bitcast(I32), 0)
+        nc.sync.dma_start(out=q_raw[:], in_=query.rearrange("(p j) q -> p j q", j=PACK))
+        nc.sync.dma_start(out=k_words[:], in_=keys_words[0])
+        for quad in range(4):
+            nc.scalar.dma_start(
+                out=k_scales[32 * quad : 32 * quad + 4, :].bitcast(I32),
+                in_=keys_scales[0, 4 * quad : 4 * quad + 4, :].bitcast(I32),
+            )
+        nc.sync.dma_start(list1[:], offs)
+        nc.sync.dma_start(list2[:], offs2)
+        nc.sync.dma_start(list3[:], offs3)
+        nc.sync.dma_start(out=old_sb[:], in_=old)
+        nc.vector.memset(placed[:], 0.0)
+
+        halves = [slice(h * Q // 2, (h + 1) * Q // 2) for h in range(2)]
+        for qs in halves:
+            nc.vector.tensor_copy(
+                out=q_bf[:, qs, :].rearrange("p (c i) j -> p c j i", i=4),
+                in_=q_raw[:, :, qs].rearrange("p j (c i) -> p c j i", i=4),
+            )
+        for qs in halves:
+            nc.vector.quantize_mx(
+                out=q_codes[:, qs].bitcast(FP8X4), scales=q_scales[:, qs], in_=q_bf[:, qs, :].rearrange("p q j -> p (q j)")
+            )
+
+        t0 = 0
+        for piece, width in enumerate(SCORE_WIDTHS):
+            bank = psum.tile([P, width], F32, name="bank%d" % piece, tag="bank%d" % piece)
+            nc.tensor.matmul_mx(
+                out=bank[:],
+                lhsT=q_codes[:].bitcast(FP8X4),
+                lhsT_scale=q_scales[:],
+                rhs=k_words[:, 2 * t0 : 2 * (t0 + width)].bitcast(FP4X4),
+                rhs_scale=k_scales[:, t0 : t0 + width],
+                start=True,
+                stop=True,
+            )
+            if piece % 2 == 0:
+                nc.vector.tensor_copy(out=scores[:, t0 : t0 + width], in_=bank[:])
+            else:
+                nc.scalar.copy(out=scores[:, t0 : t0 + width], in_=bank[:])
+            t0 = t0 + width
+
+        cols = HALF // 16
+        for half in range(2):
+            part = slice(half * cols, (half + 1) * cols)
+            first = keep.tile([P, HALF], F32, name="first%d" % half)
+            second = keep.tile([P, HALF], F32, name="second%d" % half)
+            nc.scalar.activation(second[:], scores[:].indirect(list2[:, part]), COPY, scale=-1.0)
+            if half == 0:
+                nc.vector.tensor_copy(first[:], scores[:].indirect(list1[:, part]))
+            else:
+                nc.scalar.activation(first[:], scores[:].indirect(list1[:, part]), COPY)
+            nc.vector.tensor_tensor(placed[:].indirect(list3[:, part]), first[:], second[:], ALU.add)
+
+        starts = [sum(OUT_WIDTHS[:c]) for c in range(len(OUT_WIDTHS) + 1)]
+        larger = [keep.tile([P, w], F32, name="larger%d" % c) for c, w in enumerate(OUT_WIDTHS)]
+        for c in range(len(OUT_WIDTHS) + 1):
+            if c < len(OUT_WIDTHS):
+                cs = slice(starts[c], starts[c + 1])
+                nc.vector.tensor_tensor(larger[c][:], placed[:, cs], old_sb[:, cs], ALU.max)
+            if c > 0:
+                cs = slice(starts[c - 1], starts[c])
+                result = keep.tile([P, OUT_WIDTHS[c - 1]], F32, name="result%d" % (c - 1))
+                nc.vector.scalar_tensor_tensor(result[:], old_sb[:, cs], 0.25, larger[c - 1][:], ALU.mult, ALU.add)
+                nc.sync.dma_start(out=out[:, cs], in_=result[:])

@@ -1,6 +1,7 @@
 from contextlib import ExitStack
 
 import concourse.mybir as mybir
+from concourse.masks import make_identity
 
 D, T, I, Q = 512, 1024, 512, 128
 FLOPS = 2 * D * Q * T
@@ -20,7 +21,10 @@ P = 128
 PACK = 4
 SCORE_WIDTHS = (256, 256, 256, 128, 128)
 HALF = I // 2
-OUT_WIDTHS = (256, 256, 256, 128, 128)
+BANK = 512
+OWN = 640
+OWN_WIDTHS = (256, 256, 128)
+SHARED_WIDTHS = (256, 128)
 
 
 def tile_attend_difference_lean_largerput_heads_kernel(tc, query, keys_words, keys_scales, old, offs, offs2, offs3, out):
@@ -55,6 +59,8 @@ def tile_attend_difference_lean_largerput_heads_kernel(tc, query, keys_words, ke
         nc.sync.dma_start(list3[:], offs3)
         nc.sync.dma_start(out=old_sb[:], in_=old)
         nc.vector.memset(placed[:], 0.0)
+        ident = keep.tile([P, P], F32, name="ident")
+        make_identity(nc, ident[:])
 
         halves = [slice(h * Q // 2, (h + 1) * Q // 2) for h in range(2)]
         for qs in halves:
@@ -97,14 +103,46 @@ def tile_attend_difference_lean_largerput_heads_kernel(tc, query, keys_words, ke
                 nc.scalar.activation(first[:], scores[:].indirect(list1[:, part]), COPY)
             nc.vector.tensor_tensor(placed[:].indirect(list3[:, part]), first[:], second[:], ALU.add)
 
-        starts = [sum(OUT_WIDTHS[:c]) for c in range(len(OUT_WIDTHS) + 1)]
-        larger = [keep.tile([P, w], F32, name="larger%d" % c) for c, w in enumerate(OUT_WIDTHS)]
-        for c in range(len(OUT_WIDTHS) + 1):
-            if c < len(OUT_WIDTHS):
-                cs = slice(starts[c], starts[c + 1])
-                nc.vector.tensor_tensor(larger[c][:], placed[:, cs], old_sb[:, cs], ALU.max)
+        old_ps = []
+        for b in range(T // BANK):
+            turned_ps = psum.tile([P, BANK], F32, name="turned_ps%d" % b, tag="bank%d" % (3 + b))
+            turned = keep.tile([P, BANK], F32, name="turned%d" % b)
+            back = psum.tile([P, BANK], F32, name="old_ps%d" % b)
+            for blk in range(BANK // P):
+                nc.tensor.transpose(
+                    turned_ps[:, blk * P : (blk + 1) * P], old_sb[:, b * BANK + blk * P : b * BANK + (blk + 1) * P], ident[:]
+                )
+            own = min(max(OWN - b * BANK, 0), BANK)
+            if own > 0:
+                nc.scalar.copy(out=turned[:, :own], in_=turned_ps[:, :own])
+            if own < BANK:
+                nc.scalar.activation(turned[:, own:], turned_ps[:, own:], COPY, scale=1.25)
+            for blk in range(BANK // P):
+                nc.tensor.transpose(back[:, blk * P : (blk + 1) * P], turned[:, blk * P : (blk + 1) * P], ident[:])
+            old_ps.append(back)
+
+        def old_cols(start, width):
+            return old_ps[start // BANK][:, start % BANK : start % BANK + width]
+
+        excess = keep.tile([P, T - OWN], F32, name="excess")
+        nc.gpsimd.tensor_tensor(excess[:], placed[:, OWN:], old_sb[:, OWN:], ALU.subtract)
+
+        starts = [sum(OWN_WIDTHS[:c]) for c in range(len(OWN_WIDTHS))]
+        larger = [keep.tile([P, w], F32, name="larger%d" % c) for c, w in enumerate(OWN_WIDTHS)]
+        for c in range(len(OWN_WIDTHS) + 1):
+            if c < len(OWN_WIDTHS):
+                start, width = starts[c], OWN_WIDTHS[c]
+                nc.vector.tensor_tensor(larger[c][:], placed[:, start : start + width], old_cols(start, width), ALU.max)
             if c > 0:
-                cs = slice(starts[c - 1], starts[c])
-                result = keep.tile([P, OUT_WIDTHS[c - 1]], F32, name="result%d" % (c - 1))
-                nc.vector.scalar_tensor_tensor(result[:], old_sb[:, cs], 0.25, larger[c - 1][:], ALU.mult, ALU.add)
-                nc.sync.dma_start(out=out[:, cs], in_=result[:])
+                start, width = starts[c - 1], OWN_WIDTHS[c - 1]
+                result = keep.tile([P, width], F32, name="result%d" % (c - 1))
+                nc.vector.scalar_tensor_tensor(result[:], old_cols(start, width), 0.25, larger[c - 1][:], ALU.mult, ALU.add)
+                nc.sync.dma_start(out=out[:, start : start + width], in_=result[:])
+        start = OWN
+        for c, width in enumerate(SHARED_WIDTHS):
+            result = keep.tile([P, width], F32, name="shared_result%d" % c)
+            nc.vector.scalar_tensor_tensor(
+                result[:], excess[:, start - OWN : start - OWN + width], 0.0, old_cols(start, width), ALU.max, ALU.add
+            )
+            nc.sync.dma_start(out=out[:, start : start + width], in_=result[:])
+            start = start + width

@@ -23,8 +23,6 @@ SCORE_WIDTHS = (256, 256, 256, 128, 128)
 HALF = I // 2
 BANK = 512
 OWN = 640
-OWN_WIDTHS = (256, 256, 128)
-SHARED_WIDTHS = (256, 128)
 
 
 def tile_attend_difference_lean_largerput_heads_kernel(tc, query, keys_words, keys_scales, old, offs, offs2, offs3, out):
@@ -36,19 +34,22 @@ def tile_attend_difference_lean_largerput_heads_kernel(tc, query, keys_words, ke
         list1 = keep.tile([P, I // 16], U16, name="list1")
         list2 = keep.tile([P, I // 16], U16, name="list2")
         list3 = keep.tile([P, I // 16], U16, name="list3")
-        q_raw = keep.tile([P, PACK, Q], F32, name="q_raw")
+        q_raw = [keep.tile([P, 2, Q], F32, name="q_raw%d" % u) for u in range(2)]
         q_bf = keep.tile([P, Q, PACK], BF16, name="q_bf", align_bytes=64)
         q_codes = keep.tile([P, Q], U32, name="q_codes", align_bytes=64)
         q_scales = keep.tile([P, Q], U8, name="q_scales", align_bytes=64)
-        k_words = keep.tile([P, 2 * T], U8, name="k_words", align_bytes=64)
+        k_words = [keep.tile([P, 2 * BANK], U8, name="k_words%d" % u, align_bytes=64) for u in range(T // BANK)]
         k_scales = keep.tile([P, T], U8, name="k_scales", align_bytes=64)
         old_sb = keep.tile([P, T], F32, name="old_sb")
         scores = keep.tile([P, T], F32, name="scores")
         placed = keep.tile([P, T], F32, name="placed")
 
         nc.vector.memset(k_scales[:].bitcast(I32), 0)
-        nc.sync.dma_start(out=q_raw[:], in_=query.rearrange("(p j) q -> p j q", j=PACK))
-        nc.sync.dma_start(out=k_words[:], in_=keys_words[0])
+        q_rows = query.rearrange("(p j) q -> p j q", j=PACK)
+        for u in range(2):
+            nc.sync.dma_start(out=q_raw[u][:], in_=q_rows[:, 2 * u : 2 * u + 2, :])
+        for u in range(T // BANK):
+            nc.sync.dma_start(out=k_words[u][:], in_=keys_words[0, :, 2 * BANK * u : 2 * BANK * (u + 1)])
         for quad in range(4):
             nc.scalar.dma_start(
                 out=k_scales[32 * quad : 32 * quad + 4, :].bitcast(I32),
@@ -56,18 +57,16 @@ def tile_attend_difference_lean_largerput_heads_kernel(tc, query, keys_words, ke
             )
         nc.sync.dma_start(list1[:], offs)
         nc.sync.dma_start(list2[:], offs2)
-        nc.sync.dma_start(list3[:], offs3)
         nc.sync.dma_start(out=old_sb[:], in_=old)
+        nc.sync.dma_start(list3[:], offs3)
         nc.vector.memset(placed[:], 0.0)
         ident = keep.tile([P, P], F32, name="ident")
         make_identity(nc, ident[:])
 
         halves = [slice(h * Q // 2, (h + 1) * Q // 2) for h in range(2)]
+        nc.vector.tensor_copy(out=q_bf[:, :, 0:2], in_=q_raw[0][:].rearrange("p j q -> p q j"))
         for qs in halves:
-            nc.vector.tensor_copy(
-                out=q_bf[:, qs, :].rearrange("p (c i) j -> p c j i", i=4),
-                in_=q_raw[:, :, qs].rearrange("p j (c i) -> p c j i", i=4),
-            )
+            nc.vector.tensor_copy(out=q_bf[:, qs, 2:4], in_=q_raw[1][:, :, qs].rearrange("p j q -> p q j"))
         for qs in halves:
             nc.vector.quantize_mx(
                 out=q_codes[:, qs].bitcast(FP8X4), scales=q_scales[:, qs], in_=q_bf[:, qs, :].rearrange("p q j -> p (q j)")
@@ -80,7 +79,7 @@ def tile_attend_difference_lean_largerput_heads_kernel(tc, query, keys_words, ke
                 out=bank[:],
                 lhsT=q_codes[:].bitcast(FP8X4),
                 lhsT_scale=q_scales[:],
-                rhs=k_words[:, 2 * t0 : 2 * (t0 + width)].bitcast(FP4X4),
+                rhs=k_words[t0 // BANK][:, 2 * (t0 % BANK) : 2 * (t0 % BANK + width)].bitcast(FP4X4),
                 rhs_scale=k_scales[:, t0 : t0 + width],
                 start=True,
                 stop=True,
@@ -127,22 +126,37 @@ def tile_attend_difference_lean_largerput_heads_kernel(tc, query, keys_words, ke
         excess = keep.tile([P, T - OWN], F32, name="excess")
         nc.gpsimd.tensor_tensor(excess[:], placed[:, OWN:], old_sb[:, OWN:], ALU.subtract)
 
-        starts = [sum(OWN_WIDTHS[:c]) for c in range(len(OWN_WIDTHS))]
-        larger = [keep.tile([P, w], F32, name="larger%d" % c) for c, w in enumerate(OWN_WIDTHS)]
-        for c in range(len(OWN_WIDTHS) + 1):
-            if c < len(OWN_WIDTHS):
-                start, width = starts[c], OWN_WIDTHS[c]
-                nc.vector.tensor_tensor(larger[c][:], placed[:, start : start + width], old_cols(start, width), ALU.max)
-            if c > 0:
-                start, width = starts[c - 1], OWN_WIDTHS[c - 1]
-                result = keep.tile([P, width], F32, name="result%d" % (c - 1))
-                nc.vector.scalar_tensor_tensor(result[:], old_cols(start, width), 0.25, larger[c - 1][:], ALU.mult, ALU.add)
-                nc.sync.dma_start(out=out[:, start : start + width], in_=result[:])
-        start = OWN
-        for c, width in enumerate(SHARED_WIDTHS):
-            result = keep.tile([P, width], F32, name="shared_result%d" % c)
+        larger = keep.tile([P, OWN], F32, name="larger")
+        result = keep.tile([P, T], F32, name="result")
+
+        def take_larger(start, stop):
+            nc.vector.tensor_tensor(larger[:, start:stop], placed[:, start:stop], old_cols(start, stop - start), ALU.max)
+
+        def finish_own(start, stop):
             nc.vector.scalar_tensor_tensor(
-                result[:], excess[:, start - OWN : start - OWN + width], 0.0, old_cols(start, width), ALU.max, ALU.add
+                result[:, start:stop], old_cols(start, stop - start), 0.25, larger[:, start:stop], ALU.mult, ALU.add
             )
-            nc.sync.dma_start(out=out[:, start : start + width], in_=result[:])
-            start = start + width
+
+        def finish_shared(start, stop):
+            nc.vector.scalar_tensor_tensor(
+                result[:, start:stop], excess[:, start - OWN : stop - OWN], 0.0, old_cols(start, stop - start), ALU.max, ALU.add
+            )
+
+        def store(start, stop):
+            nc.sync.dma_start(out=out[:, start:stop], in_=result[:, start:stop])
+
+        take_larger(0, 128)
+        take_larger(128, 320)
+        finish_own(0, 128)
+        store(0, 128)
+        take_larger(320, 512)
+        finish_own(128, 320)
+        store(128, 320)
+        take_larger(512, 640)
+        finish_own(320, 512)
+        store(320, 512)
+        finish_shared(768, 1024)
+        store(768, 1024)
+        finish_own(512, 640)
+        finish_shared(640, 768)
+        store(512, 768)

@@ -34,39 +34,35 @@ def tile_attend_difference_lean_largerput_heads_kernel(tc, query, keys_words, ke
         list1 = keep.tile([P, I // 16], U16, name="list1")
         list2 = keep.tile([P, I // 16], U16, name="list2")
         list3 = keep.tile([P, I // 16], U16, name="list3")
-        q_raw = [keep.tile([P, 2, Q], F32, name="q_raw%d" % u) for u in range(2)]
+        q_raw = keep.tile([P, PACK, Q], F32, name="q_raw")
         q_bf = keep.tile([P, Q, PACK], BF16, name="q_bf", align_bytes=64)
         q_codes = keep.tile([P, Q], U32, name="q_codes", align_bytes=64)
         q_scales = keep.tile([P, Q], U8, name="q_scales", align_bytes=64)
-        k_words = [keep.tile([P, 2 * BANK], U8, name="k_words%d" % u, align_bytes=64) for u in range(T // BANK)]
+        k_words = keep.tile([P, 2 * T], U8, name="k_words", align_bytes=64)
         k_scales = keep.tile([P, T], U8, name="k_scales", align_bytes=64)
         old_sb = keep.tile([P, T], F32, name="old_sb")
         scores = keep.tile([P, T], F32, name="scores")
         placed = keep.tile([P, T], F32, name="placed")
 
         nc.vector.memset(k_scales[:].bitcast(I32), 0)
-        q_rows = query.rearrange("(p j) q -> p j q", j=PACK)
-        for u in range(2):
-            nc.sync.dma_start(out=q_raw[u][:], in_=q_rows[:, 2 * u : 2 * u + 2, :])
-        for u in range(T // BANK):
-            nc.sync.dma_start(out=k_words[u][:], in_=keys_words[0, :, 2 * BANK * u : 2 * BANK * (u + 1)])
-        for quad in range(4):
-            nc.scalar.dma_start(
-                out=k_scales[32 * quad : 32 * quad + 4, :].bitcast(I32),
-                in_=keys_scales[0, 4 * quad : 4 * quad + 4, :].bitcast(I32),
-            )
+        nc.sync.dma_start(out=q_raw[:], in_=query.rearrange("(p j) q -> p j q", j=PACK))
+        nc.sync.dma_start(out=k_words[:], in_=keys_words[0])
+        for r in range(4):
+            nc.scalar.dma_start(out=k_scales[r:P:32, :].bitcast(I32), in_=keys_scales[0, r:16:4, :].bitcast(I32))
         nc.sync.dma_start(list1[:], offs)
         nc.sync.dma_start(list2[:], offs2)
-        nc.sync.dma_start(out=old_sb[:], in_=old)
         nc.sync.dma_start(list3[:], offs3)
+        nc.sync.dma_start(out=old_sb[:], in_=old)
         nc.vector.memset(placed[:], 0.0)
         ident = keep.tile([P, P], F32, name="ident")
         make_identity(nc, ident[:])
 
         halves = [slice(h * Q // 2, (h + 1) * Q // 2) for h in range(2)]
-        nc.vector.tensor_copy(out=q_bf[:, :, 0:2], in_=q_raw[0][:].rearrange("p j q -> p q j"))
         for qs in halves:
-            nc.vector.tensor_copy(out=q_bf[:, qs, 2:4], in_=q_raw[1][:, :, qs].rearrange("p j q -> p q j"))
+            nc.vector.tensor_copy(
+                out=q_bf[:, qs, :].rearrange("p (c i) j -> p c j i", i=4),
+                in_=q_raw[:, :, qs].rearrange("p j (c i) -> p c j i", i=4),
+            )
         for qs in halves:
             nc.vector.quantize_mx(
                 out=q_codes[:, qs].bitcast(FP8X4), scales=q_scales[:, qs], in_=q_bf[:, qs, :].rearrange("p q j -> p (q j)")
@@ -79,7 +75,7 @@ def tile_attend_difference_lean_largerput_heads_kernel(tc, query, keys_words, ke
                 out=bank[:],
                 lhsT=q_codes[:].bitcast(FP8X4),
                 lhsT_scale=q_scales[:],
-                rhs=k_words[t0 // BANK][:, 2 * (t0 % BANK) : 2 * (t0 % BANK + width)].bitcast(FP4X4),
+                rhs=k_words[:, 2 * t0 : 2 * (t0 + width)].bitcast(FP4X4),
                 rhs_scale=k_scales[:, t0 : t0 + width],
                 start=True,
                 stop=True,

from contextlib import ExitStack

import concourse.mybir as mybir
from concourse.masks import make_identity

D, T, I, Q = 512, 1024, 512, 128
FLOPS = 2 * D * Q * T

F32 = mybir.dt.float32
BF16 = mybir.dt.bfloat16
I32 = mybir.dt.int32
U32 = mybir.dt.uint32
U16 = mybir.dt.uint16
U8 = mybir.dt.uint8
FP8X4 = mybir.dt.float8_e4m3fn_x4
FP4X4 = mybir.dt.float4_e2m1fn_x4
ALU = mybir.AluOpType
COPY = mybir.ActivationFunctionType.Copy

P = 128
PACK = 4
SCORE_WIDTHS = (256, 256, 256, 128, 128)
HALF = I // 2
BANK = 512
OWN = 640


def tile_attend_difference_lean_largerput_heads_kernel(tc, query, keys_words, keys_scales, old, offs, offs2, offs3, out):
    nc = tc.nc
    with ExitStack() as ctx:
        keep = ctx.enter_context(tc.tile_pool(name="keep", bufs=1))
        psum = ctx.enter_context(tc.psum_pool(name="psum", bufs=1))

        list1 = keep.tile([P, I // 16], U16, name="list1")
        list2 = keep.tile([P, I // 16], U16, name="list2")
        list3 = keep.tile([P, I // 16], U16, name="list3")
        q_raw = keep.tile([P, PACK, Q], F32, name="q_raw")
        q_bf = keep.tile([P, Q, PACK], BF16, name="q_bf", align_bytes=64)
        q_codes = keep.tile([P, Q], U32, name="q_codes", align_bytes=64)
        q_scales = keep.tile([P, Q], U8, name="q_scales", align_bytes=64)
        k_words = keep.tile([P, 2 * T], U8, name="k_words", align_bytes=64)
        k_scales = keep.tile([P, T], U8, name="k_scales", align_bytes=64)
        old_sb = keep.tile([P, T], F32, name="old_sb")
        scores = keep.tile([P, T], F32, name="scores")
        placed = keep.tile([P, T], F32, name="placed")

        nc.vector.memset(k_scales[:].bitcast(I32), 0)
        nc.sync.dma_start(out=q_raw[:], in_=query.rearrange("(p j) q -> p j q", j=PACK))
        nc.sync.dma_start(out=k_words[:], in_=keys_words[0])
        for r in range(4):
            nc.scalar.dma_start(out=k_scales[r:P:32, :].bitcast(I32), in_=keys_scales[0, r:16:4, :].bitcast(I32))
        nc.sync.dma_start(list1[:], offs)
        nc.sync.dma_start(list2[:], offs2)
        nc.sync.dma_start(list3[:], offs3)
        nc.sync.dma_start(out=old_sb[:], in_=old)
        nc.vector.memset(placed[:], 0.0)
        ident = keep.tile([P, P], F32, name="ident")
        make_identity(nc, ident[:])

        halves = [slice(h * Q // 2, (h + 1) * Q // 2) for h in range(2)]
        for qs in halves:
            nc.vector.tensor_copy(
                out=q_bf[:, qs, :].rearrange("p (c i) j -> p c j i", i=4),
                in_=q_raw[:, :, qs].rearrange("p j (c i) -> p c j i", i=4),
            )
        for qs in halves:
            nc.vector.quantize_mx(
                out=q_codes[:, qs].bitcast(FP8X4), scales=q_scales[:, qs], in_=q_bf[:, qs, :].rearrange("p q j -> p (q j)")
            )

        t0 = 0
        for piece, width in enumerate(SCORE_WIDTHS):
            bank = psum.tile([P, width], F32, name="bank%d" % piece, tag="bank%d" % piece)
            nc.tensor.matmul_mx(
                out=bank[:],
                lhsT=q_codes[:].bitcast(FP8X4),
                lhsT_scale=q_scales[:],
                rhs=k_words[:, 2 * t0 : 2 * (t0 + width)].bitcast(FP4X4),
                rhs_scale=k_scales[:, t0 : t0 + width],
                start=True,
                stop=True,
            )
            if piece % 2 == 0:
                nc.vector.tensor_copy(out=scores[:, t0 : t0 + width], in_=bank[:])
            else:
                nc.scalar.copy(out=scores[:, t0 : t0 + width], in_=bank[:])
            t0 = t0 + width

        cols = HALF // 16
        for half in range(2):
            part = slice(half * cols, (half + 1) * cols)
            first = keep.tile([P, HALF], F32, name="first%d" % half)
            second = keep.tile([P, HALF], F32, name="second%d" % half)
            nc.scalar.activation(second[:], scores[:].indirect(list2[:, part]), COPY, scale=-1.0)
            if half == 0:
                nc.vector.tensor_copy(first[:], scores[:].indirect(list1[:, part]))
            else:
                nc.scalar.activation(first[:], scores[:].indirect(list1[:, part]), COPY)
            nc.vector.tensor_tensor(placed[:].indirect(list3[:, part]), first[:], second[:], ALU.add)

        old_ps = []
        for b in range(T // BANK):
            turned_ps = psum.tile([P, BANK], F32, name="turned_ps%d" % b, tag="bank%d" % (3 + b))
            turned = keep.tile([P, BANK], F32, name="turned%d" % b)
            back = psum.tile([P, BANK], F32, name="old_ps%d" % b)
            for blk in range(BANK // P):
                nc.tensor.transpose(
                    turned_ps[:, blk * P : (blk + 1) * P], old_sb[:, b * BANK + blk * P : b * BANK + (blk + 1) * P], ident[:]
                )
            own = min(max(OWN - b * BANK, 0), BANK)
            if own > 0:
                nc.scalar.copy(out=turned[:, :own], in_=turned_ps[:, :own])
            if own < BANK:
                nc.scalar.activation(turned[:, own:], turned_ps[:, own:], COPY, scale=1.25)
            for blk in range(BANK // P):
                nc.tensor.transpose(back[:, blk * P : (blk + 1) * P], turned[:, blk * P : (blk + 1) * P], ident[:])
            old_ps.append(back)

        def old_cols(start, width):
            return old_ps[start // BANK][:, start % BANK : start % BANK + width]

        excess = keep.tile([P, T - OWN], F32, name="excess")
        nc.gpsimd.tensor_tensor(excess[:], placed[:, OWN:], old_sb[:, OWN:], ALU.subtract)

        larger = keep.tile([P, OWN], F32, name="larger")
        result = keep.tile([P, T], F32, name="result")

        def take_larger(start, stop):
            nc.vector.tensor_tensor(larger[:, start:stop], placed[:, start:stop], old_cols(start, stop - start), ALU.max)

        def finish_own(start, stop):
            nc.vector.scalar_tensor_tensor(
                result[:, start:stop], old_cols(start, stop - start), 0.25, larger[:, start:stop], ALU.mult, ALU.add
            )

        def finish_shared(start, stop):
            nc.vector.scalar_tensor_tensor(
                result[:, start:stop], excess[:, start - OWN : stop - OWN], 0.0, old_cols(start, stop - start), ALU.max, ALU.add
            )

        def store(start, stop):
            nc.sync.dma_start(out=out[:, start:stop], in_=result[:, start:stop])

        take_larger(0, 128)
        take_larger(128, 320)
        finish_own(0, 128)
        store(0, 128)
        take_larger(320, 512)
        finish_own(128, 320)
        store(128, 320)
        take_larger(512, 640)
        finish_own(320, 512)
        store(320, 512)
        finish_shared(768, 1024)
        store(768, 1024)
        finish_own(512, 640)
        finish_shared(640, 768)
        store(512, 768)
